import numpy as np
import ml_dtypes


def mxq(x, axis, fmt="e4m3"):
    dtype, down = {"e4m3": (ml_dtypes.float8_e4m3fn, 7), "e5m2": (ml_dtypes.float8_e5m2, 14)}[fmt]
    v = np.moveaxis(np.asarray(x, np.float32).astype(ml_dtypes.bfloat16).astype(np.float64), axis, -1)
    blocks = v.reshape(v.shape[:-1] + (-1, 32))
    amax = np.abs(blocks).max(-1, keepdims=True)
    byte = np.maximum(np.where(amax > 0, np.frexp(amax)[1] - 1 + 127, 0) - down, 1)
    scale = np.exp2(byte - 127.0)
    codes = (blocks / scale).astype(np.float32).astype(dtype).astype(np.float64)
    return np.moveaxis((codes * scale).reshape(v.shape), -1, axis)


WIDE = False


def mx_kscale(k):
    if not WIDE:
        return np.ones(k)
    levels = np.array([10, -10, 5, -5, 0])
    if k % 512:
        return np.exp2(np.random.permutation(np.resize(levels, k // 32))).repeat(32)
    a = np.empty((k // 512, 16))
    for p in range(k // 512):
        a[p, :8] = np.random.permutation(np.resize(levels, 8))
        for g in range(8):
            far = levels[np.abs(levels - a[p, g]) >= 10]
            a[p, g + 8] = far[np.random.randint(len(far))]
    return np.exp2(a.ravel()).repeat(32)


def f64(x):
    return np.asarray(x).astype(np.float64)


def striped8(idx):
    return np.concatenate([v.reshape(-1, 16).T for v in idx]).astype(np.uint16)


def unstriped8(offs):
    return np.stack([offs[16 * g:16 * g + 16].T.reshape(-1) for g in range(8)]).astype(np.int64)


def silu(v):
    return v / (1.0 + np.exp(-np.maximum(v, -700.0)))


K, M, T, S = 512, 256, 2048, 1024


def setup_inputs():
    n = np.random.standard_normal
    s = mx_kscale(K)[:, None]
    return {
        "xT": (n((K, T)) * s).astype(np.float32),
        "w": (n((K, M)) / np.sqrt(K) / s).astype(np.float32),
        "wgt": np.repeat(np.random.uniform(0.5, 2.0, (8, S)), 16, axis=0).astype(np.float32),
        "b": (0.3 * n(256)).astype(np.float32),
        "wgo": np.repeat(np.random.uniform(0.5, 2.0, (8, S)), 16, axis=0).astype(np.float32),
        "offs": striped8(np.stack([np.random.permutation(T)[:S] for _ in range(8)])),
        "offs2": striped8(np.stack([np.random.permutation(T)[:S] for _ in range(8)])),
    }


def reference(xT, w, wgt, b, wgo, offs, offs2):
    idx = unstriped8(offs)
    group = np.arange(K) % 512 // 64
    xg = f64(wgt)[np.arange(K) // 4 % 128] * f64(xT)[np.arange(K)[:, None], idx[group]]
    xT_ = mxq(xg, 0, "e4m3")
    w_ = mxq(f64(w), 0, "e4m3")
    y = w_.T @ xT_
    place = unstriped8(offs2)[np.arange(M) % 128 // 16]
    out = np.zeros((M, T))
    out[np.arange(M)[:, None], place] = f64(wgo)[np.arange(M) % 128] * (silu(y + f64(b)[:, None]))
    return out

@@ -1,0 +1,145 @@
+from contextlib import ExitStack
+
+import concourse.mybir as mybir
+
+K, M, T, S = 512, 256, 2048, 1024
+FLOPS = 2 * K * M * S
+
+F32 = mybir.dt.float32
+BF16 = mybir.dt.bfloat16
+U32 = mybir.dt.uint32
+U16 = mybir.dt.uint16
+U8 = mybir.dt.uint8
+FP8X4 = mybir.dt.float8_e4m3fn_x4
+MULT = mybir.AluOpType.mult
+SILU = mybir.ActivationFunctionType.Silu
+
+P = 128
+PACK = 4
+HALF = S // 2
+LIST_ROWS = 16
+
+
+def tile_list_hboth_silu_kernel(tc, xT, w, wgt, b, wgo, offs, offs2, out):
+    nc = tc.nc
+    with ExitStack() as ctx:
+        keep = ctx.enter_context(tc.tile_pool(name="keep", bufs=1))
+        psum = ctx.enter_context(tc.psum_pool(name="psum", bufs=1))
+
+        offs_t = keep.tile([P, S // LIST_ROWS], U16, name="offs_t")
+        offs2_t = keep.tile([P, S // LIST_ROWS], U16, name="offs2_t")
+        planes = [keep.tile([P, T], F32, name=f"plane{i}") for i in range(PACK)]
+        wgt_t = keep.tile([P, S], F32, name="wgt_t")
+        w_raw = keep.tile([P, PACK, M], F32, name="w_raw")
+        wgo_t = keep.tile([P, S], F32, name="wgo_t")
+        b_t = keep.tile([P, 2], F32, name="b_t")
+        picked = [keep.tile([P, PACK, HALF], F32, name=f"picked{h}") for h in range(2)]
+        grouped = [keep.tile([P, HALF, PACK], BF16, name=f"grouped{h}", align_bytes=64) for h in range(2)]
+        codes = [keep.tile([P, HALF], U32, name=f"codes{h}", align_bytes=64) for h in range(2)]
+        scales = [keep.tile([P, HALF], U8, name=f"scales{h}", align_bytes=64) for h in range(2)]
+        w_grouped = keep.tile([P, M, PACK], BF16, name="w_grouped", align_bytes=64)
+        w_codes = keep.tile([P, M], U32, name="w_codes", align_bytes=64)
+        w_scales = keep.tile([P, M], U8, name="w_scales", align_bytes=64)
+        windows = [keep.tile([P, T], F32, name=f"window{r}") for r in range(2)]
+        y = [[keep.tile([P, HALF], F32, name=f"y{r}{h}") for h in range(2)] for r in range(2)]
+        warm = keep.tile([P, 1], F32, name="warm")
+
+        x_planes = xT.rearrange("(p i) t -> p i t", i=PACK)
+        nc.sync.dma_start(offs_t[:], offs)
+        nc.sync.dma_start(wgt_t[:, 0:P], wgt[:, 0:P])
+        nc.sync.dma_start(planes[0][:], x_planes[:, 0, :])
+        nc.sync.dma_start(wgt_t[:, P:HALF], wgt[:, P:HALF])
+        nc.sync.dma_start(wgt_t[:, HALF:S], wgt[:, HALF:S])
+        with nc.allow_non_contiguous_dma(reason="bias, one value to a partition"):
+            nc.scalar.dma_start(b_t[:], b.rearrange("(r p) -> p r", p=P))
+        for i in range(1, PACK):
+            nc.sync.dma_start(planes[i][:], x_planes[:, i, :])
+        nc.sync.dma_start(w_raw[:], w.rearrange("(p i) m -> p i m", i=PACK))
+        nc.sync.dma_start(offs2_t[:], offs2)
+        nc.sync.dma_start(wgo_t[:], wgo)
+
+        nc.vector.memset(warm[:], 0.0)
+        nc.scalar.activation(warm[:], warm[:], SILU)
+        nc.vector.memset(windows[0][:], 0.0)
+        nc.gpsimd.memset(windows[1][:], 0.0)
+
+        def gather(i, h, c0, c1):
+            j0, j1 = h * HALF + c0, h * HALF + c1
+            nc.vector.tensor_tensor(
+                picked[h][:, i, c0:c1],
+                planes[i][:].indirect(offs_t[:, j0 // LIST_ROWS : j1 // LIST_ROWS]),
+                wgt_t[:, j0:j1],
+                MULT,
+            )
+
+        def interleave(pair, h, c0, c1):
+            i0 = 2 * pair
+            nc.scalar.copy(
+                grouped[h][:, c0:c1, i0 : i0 + 2],
+                picked[h][:, i0 : i0 + 2, c0:c1].rearrange("p i n -> p n i"),
+            )
+
+        def quantize(h, c0, c1):
+            nc.vector.quantize_mx(
+                out=codes[h][:, c0:c1].bitcast(FP8X4),
+                scales=scales[h][:, c0:c1],
+                in_=grouped[h][:, c0:c1, :].rearrange("p n i -> p (n i)"),
+            )
+
+        def product(r, h, c0, c1):
+            rows = slice(r * P, (r + 1) * P)
+            bank = psum.tile([P, c1 - c0], F32, name=f"bank{r}_{h}_{c0}")
+            nc.tensor.matmul_mx(
+                out=bank[:],
+                lhsT=w_codes[:, rows].bitcast(FP8X4),
+                lhsT_scale=w_scales[:, rows],
+                rhs=codes[h][:, c0:c1].bitcast(FP8X4),
+                rhs_scale=scales[h][:, c0:c1],
+                start=True,
+                stop=True,
+            )
+            nc.scalar.activation(y[r][h][:, c0:c1], bank[:], SILU, bias=b_t[:, r : r + 1])
+
+        def scatter(r, h):
+            cols = slice(h * HALF, (h + 1) * HALF)
+            nc.vector.tensor_tensor(
+                windows[r][:].indirect(offs2_t[:, h * HALF // LIST_ROWS : (h + 1) * HALF // LIST_ROWS]),
+                y[r][h][:],
+                wgo_t[:, cols],
+                MULT,
+            )
+
+        Q = HALF // 2
+        for i in range(3):
+            for h in range(2):
+                if i == 0 and h == 0:
+                    gather(i, h, 0, P)
+                    gather(i, h, P, HALF)
+                else:
+                    gather(i, h, 0, HALF)
+                if i == 1:
+                    interleave(0, h, 0, HALF)
+        gather(3, 0, 0, Q)
+        interleave(1, 0, 0, Q)
+        gather(3, 0, Q, HALF)
+        interleave(1, 0, Q, HALF)
+        nc.vector.tensor_copy(w_grouped[:], w_raw[:].rearrange("p i m -> p m i"))
+        gather(3, 1, 0, Q)
+        nc.vector.quantize_mx(
+            out=w_codes[:].bitcast(FP8X4), scales=w_scales[:], in_=w_grouped[:].rearrange("p m i -> p (m i)")
+        )
+        quantize(0, 0, Q)
+        quantize(0, Q, HALF)
+        for r in range(2):
+            product(r, 0, 0, Q)
+            product(r, 0, Q, HALF)
+        gather(3, 1, Q, HALF)
+        interleave(1, 1, 0, HALF)
+        scatter(0, 0)
+        quantize(1, 0, HALF)
+        for r in range(2):
+            product(r, 1, 0, HALF)
+        scatter(1, 0)
+        for r in range(2):
+            scatter(r, 1)
+            nc.sync.dma_start(out[r * P : (r + 1) * P, :], windows[r][:])

@@ -50,11 +50,11 @@ def tile_list_hboth_silu_kernel(tc, xT, w, wgt, b, wgo, offs, offs2, out):
         nc.sync.dma_start(planes[0][:], x_planes[:, 0, :])
         nc.sync.dma_start(wgt_t[:, P:HALF], wgt[:, P:HALF])
         nc.sync.dma_start(wgt_t[:, HALF:S], wgt[:, HALF:S])
-        with nc.allow_non_contiguous_dma(reason="bias, one value to a partition"):
-            nc.scalar.dma_start(b_t[:], b.rearrange("(r p) -> p r", p=P))
         for i in range(1, PACK):
             nc.sync.dma_start(planes[i][:], x_planes[:, i, :])
         nc.sync.dma_start(w_raw[:], w.rearrange("(p i) m -> p i m", i=PACK))
+        with nc.allow_non_contiguous_dma(reason="bias, one value to a partition"):
+            nc.sync.dma_start(b_t[:], b.rearrange("(r p) -> p r", p=P))
         nc.sync.dma_start(offs2_t[:], offs2)
         nc.sync.dma_start(wgo_t[:], wgo)
 
@@ -124,16 +124,15 @@ def tile_list_hboth_silu_kernel(tc, xT, w, wgt, b, wgo, offs, offs2, out):
         gather(3, 0, Q, HALF)
         interleave(1, 0, Q, HALF)
         nc.vector.tensor_copy(w_grouped[:], w_raw[:].rearrange("p i m -> p m i"))
-        gather(3, 1, 0, Q)
+        quantize(0, 0, Q)
         nc.vector.quantize_mx(
             out=w_codes[:].bitcast(FP8X4), scales=w_scales[:], in_=w_grouped[:].rearrange("p m i -> p (m i)")
         )
-        quantize(0, 0, Q)
         quantize(0, Q, HALF)
         for r in range(2):
             product(r, 0, 0, Q)
             product(r, 0, Q, HALF)
-        gather(3, 1, Q, HALF)
+        gather(3, 1, 0, HALF)
         interleave(1, 1, 0, HALF)
         scatter(0, 0)
         quantize(1, 0, HALF)

@@ -37,9 +37,9 @@ def tile_list_hboth_silu_kernel(tc, xT, w, wgt, b, wgo, offs, offs2, out):
         grouped = [keep.tile([P, HALF, PACK], BF16, name=f"grouped{h}", align_bytes=64) for h in range(2)]
         codes = [keep.tile([P, HALF], U32, name=f"codes{h}", align_bytes=64) for h in range(2)]
         scales = [keep.tile([P, HALF], U8, name=f"scales{h}", align_bytes=64) for h in range(2)]
-        w_grouped = keep.tile([P, M, PACK], BF16, name="w_grouped", align_bytes=64)
-        w_codes = keep.tile([P, M], U32, name="w_codes", align_bytes=64)
-        w_scales = keep.tile([P, M], U8, name="w_scales", align_bytes=64)
+        w_grouped = [keep.tile([P, P, PACK], BF16, name=f"w_grouped{r}", align_bytes=64) for r in range(2)]
+        w_codes = [keep.tile([P, P], U32, name=f"w_codes{r}", align_bytes=64) for r in range(2)]
+        w_scales = [keep.tile([P, P], U8, name=f"w_scales{r}", align_bytes=64) for r in range(2)]
         windows = [keep.tile([P, T], F32, name=f"window{r}") for r in range(2)]
         y = [[keep.tile([P, HALF], F32, name=f"y{r}{h}") for h in range(2)] for r in range(2)]
         warm = keep.tile([P, 1], F32, name="warm")
@@ -53,10 +53,11 @@ def tile_list_hboth_silu_kernel(tc, xT, w, wgt, b, wgo, offs, offs2, out):
         for i in range(1, PACK):
             nc.sync.dma_start(planes[i][:], x_planes[:, i, :])
         nc.sync.dma_start(w_raw[:], w.rearrange("(p i) m -> p i m", i=PACK))
+        nc.sync.dma_start(offs2_t[:], offs2)
+        nc.sync.dma_start(wgo_t[:, 0:HALF], wgo[:, 0:HALF])
         with nc.allow_non_contiguous_dma(reason="bias, one value to a partition"):
             nc.sync.dma_start(b_t[:], b.rearrange("(r p) -> p r", p=P))
-        nc.sync.dma_start(offs2_t[:], offs2)
-        nc.sync.dma_start(wgo_t[:], wgo)
+        nc.sync.dma_start(wgo_t[:, HALF:S], wgo[:, HALF:S])
 
         nc.vector.memset(warm[:], 0.0)
         nc.scalar.activation(warm[:], warm[:], SILU)
@@ -72,9 +73,9 @@ def tile_list_hboth_silu_kernel(tc, xT, w, wgt, b, wgo, offs, offs2, out):
                 MULT,
             )
 
-        def interleave(pair, h, c0, c1):
+        def interleave(copy, pair, h, c0, c1):
             i0 = 2 * pair
-            nc.scalar.copy(
+            copy(
                 grouped[h][:, c0:c1, i0 : i0 + 2],
                 picked[h][:, i0 : i0 + 2, c0:c1].rearrange("p i n -> p n i"),
             )
@@ -86,13 +87,22 @@ def tile_list_hboth_silu_kernel(tc, xT, w, wgt, b, wgo, offs, offs2, out):
                 in_=grouped[h][:, c0:c1, :].rearrange("p n i -> p (n i)"),
             )
 
+        def interleave_w(copy, r):
+            copy(w_grouped[r][:], w_raw[:, :, r * P : (r + 1) * P].rearrange("p i m -> p m i"))
+
+        def quantize_w(r):
+            nc.vector.quantize_mx(
+                out=w_codes[r][:].bitcast(FP8X4),
+                scales=w_scales[r][:],
+                in_=w_grouped[r][:].rearrange("p m i -> p (m i)"),
+            )
+
         def product(r, h, c0, c1):
-            rows = slice(r * P, (r + 1) * P)
             bank = psum.tile([P, c1 - c0], F32, name=f"bank{r}_{h}_{c0}")
             nc.tensor.matmul_mx(
                 out=bank[:],
-                lhsT=w_codes[:, rows].bitcast(FP8X4),
-                lhsT_scale=w_scales[:, rows],
+                lhsT=w_codes[r][:].bitcast(FP8X4),
+                lhsT_scale=w_scales[r][:],
                 rhs=codes[h][:, c0:c1].bitcast(FP8X4),
                 rhs_scale=scales[h][:, c0:c1],
                 start=True,
@@ -118,22 +128,25 @@ def tile_list_hboth_silu_kernel(tc, xT, w, wgt, b, wgo, offs, offs2, out):
                 else:
                     gather(i, h, 0, HALF)
                 if i == 1:
-                    interleave(0, h, 0, HALF)
+                    interleave(nc.scalar.copy, 0, h, 0, HALF)
         gather(3, 0, 0, Q)
-        interleave(1, 0, 0, Q)
-        gather(3, 0, Q, HALF)
-        interleave(1, 0, Q, HALF)
-        nc.vector.tensor_copy(w_grouped[:], w_raw[:].rearrange("p i m -> p m i"))
+        interleave(nc.scalar.copy, 1, 0, 0, Q)
+        gather(3, 0, Q + P, HALF)
+        gather(3, 0, Q, Q + P)
+        interleave(nc.scalar.copy, 1, 0, Q, Q + P)
+        interleave(nc.vector.tensor_copy, 1, 0, Q + P, HALF)
+        interleave_w(nc.vector.tensor_copy, 0)
         quantize(0, 0, Q)
-        nc.vector.quantize_mx(
-            out=w_codes[:].bitcast(FP8X4), scales=w_scales[:], in_=w_grouped[:].rearrange("p m i -> p (m i)")
-        )
+        quantize_w(0)
+        interleave_w(nc.scalar.copy, 1)
         quantize(0, Q, HALF)
-        for r in range(2):
-            product(r, 0, 0, Q)
-            product(r, 0, Q, HALF)
+        product(0, 0, 0, Q)
+        product(0, 0, Q, HALF)
         gather(3, 1, 0, HALF)
-        interleave(1, 1, 0, HALF)
+        quantize_w(1)
+        product(1, 0, 0, Q)
+        product(1, 0, Q, HALF)
+        interleave(nc.scalar.copy, 1, 1, 0, HALF)
         scatter(0, 0)
         quantize(1, 0, HALF)
         for r in range(2):

from contextlib import ExitStack

import concourse.mybir as mybir

K, M, T, S = 512, 256, 2048, 1024
FLOPS = 2 * K * M * S

F32 = mybir.dt.float32
BF16 = mybir.dt.bfloat16
U32 = mybir.dt.uint32
U16 = mybir.dt.uint16
U8 = mybir.dt.uint8
FP8X4 = mybir.dt.float8_e4m3fn_x4
MULT = mybir.AluOpType.mult
SILU = mybir.ActivationFunctionType.Silu

P = 128
PACK = 4
HALF = S // 2
LIST_ROWS = 16


def tile_list_hboth_silu_kernel(tc, xT, w, wgt, b, wgo, offs, offs2, out):
    nc = tc.nc
    with ExitStack() as ctx:
        keep = ctx.enter_context(tc.tile_pool(name="keep", bufs=1))
        psum = ctx.enter_context(tc.psum_pool(name="psum", bufs=1))

        offs_t = keep.tile([P, S // LIST_ROWS], U16, name="offs_t")
        offs2_t = keep.tile([P, S // LIST_ROWS], U16, name="offs2_t")
        planes = [keep.tile([P, T], F32, name=f"plane{i}") for i in range(PACK)]
        wgt_t = keep.tile([P, S], F32, name="wgt_t")
        w_raw = keep.tile([P, PACK, M], F32, name="w_raw")
        wgo_t = keep.tile([P, S], F32, name="wgo_t")
        b_t = keep.tile([P, 2], F32, name="b_t")
        picked = [keep.tile([P, PACK, HALF], F32, name=f"picked{h}") for h in range(2)]
        grouped = [keep.tile([P, HALF, PACK], BF16, name=f"grouped{h}", align_bytes=64) for h in range(2)]
        codes = [keep.tile([P, HALF], U32, name=f"codes{h}", align_bytes=64) for h in range(2)]
        scales = [keep.tile([P, HALF], U8, name=f"scales{h}", align_bytes=64) for h in range(2)]
        w_grouped = [keep.tile([P, P, PACK], BF16, name=f"w_grouped{r}", align_bytes=64) for r in range(2)]
        w_codes = [keep.tile([P, P], U32, name=f"w_codes{r}", align_bytes=64) for r in range(2)]
        w_scales = [keep.tile([P, P], U8, name=f"w_scales{r}", align_bytes=64) for r in range(2)]
        windows = [keep.tile([P, T], F32, name=f"window{r}") for r in range(2)]
        y = [[keep.tile([P, HALF], F32, name=f"y{r}{h}") for h in range(2)] for r in range(2)]
        warm = keep.tile([P, 1], F32, name="warm")

        x_planes = xT.rearrange("(p i) t -> p i t", i=PACK)
        nc.sync.dma_start(offs_t[:], offs)
        nc.sync.dma_start(wgt_t[:, 0:P], wgt[:, 0:P])
        nc.sync.dma_start(planes[0][:], x_planes[:, 0, :])
        nc.sync.dma_start(wgt_t[:, P:HALF], wgt[:, P:HALF])
        nc.sync.dma_start(wgt_t[:, HALF:S], wgt[:, HALF:S])
        for i in range(1, PACK):
            nc.sync.dma_start(planes[i][:], x_planes[:, i, :])
        nc.sync.dma_start(w_raw[:], w.rearrange("(p i) m -> p i m", i=PACK))
        nc.sync.dma_start(offs2_t[:], offs2)
        nc.sync.dma_start(wgo_t[:, 0:HALF], wgo[:, 0:HALF])
        with nc.allow_non_contiguous_dma(reason="bias, one value to a partition"):
            nc.sync.dma_start(b_t[:], b.rearrange("(r p) -> p r", p=P))
        nc.sync.dma_start(wgo_t[:, HALF:S], wgo[:, HALF:S])

        nc.vector.memset(warm[:], 0.0)
        nc.scalar.activation(warm[:], warm[:], SILU)
        nc.vector.memset(windows[0][:], 0.0)
        nc.gpsimd.memset(windows[1][:], 0.0)

        def gather(i, h, c0, c1):
            j0, j1 = h * HALF + c0, h * HALF + c1
            nc.vector.tensor_tensor(
                picked[h][:, i, c0:c1],
                planes[i][:].indirect(offs_t[:, j0 // LIST_ROWS : j1 // LIST_ROWS]),
                wgt_t[:, j0:j1],
                MULT,
            )

        def interleave(copy, pair, h, c0, c1):
            i0 = 2 * pair
            copy(
                grouped[h][:, c0:c1, i0 : i0 + 2],
                picked[h][:, i0 : i0 + 2, c0:c1].rearrange("p i n -> p n i"),
            )

        def quantize(h, c0, c1):
            nc.vector.quantize_mx(
                out=codes[h][:, c0:c1].bitcast(FP8X4),
                scales=scales[h][:, c0:c1],
                in_=grouped[h][:, c0:c1, :].rearrange("p n i -> p (n i)"),
            )

        def interleave_w(copy, r):
            copy(w_grouped[r][:], w_raw[:, :, r * P : (r + 1) * P].rearrange("p i m -> p m i"))

        def quantize_w(r):
            nc.vector.quantize_mx(
                out=w_codes[r][:].bitcast(FP8X4),
                scales=w_scales[r][:],
                in_=w_grouped[r][:].rearrange("p m i -> p (m i)"),
            )

        def product(r, h, c0, c1):
            bank = psum.tile([P, c1 - c0], F32, name=f"bank{r}_{h}_{c0}")
            nc.tensor.matmul_mx(
                out=bank[:],
                lhsT=w_codes[r][:].bitcast(FP8X4),
                lhsT_scale=w_scales[r][:],
                rhs=codes[h][:, c0:c1].bitcast(FP8X4),
                rhs_scale=scales[h][:, c0:c1],
                start=True,
                stop=True,
            )
            nc.scalar.activation(y[r][h][:, c0:c1], bank[:], SILU, bias=b_t[:, r : r + 1])

        def scatter(r, h):
            cols = slice(h * HALF, (h + 1) * HALF)
            nc.vector.tensor_tensor(
                windows[r][:].indirect(offs2_t[:, h * HALF // LIST_ROWS : (h + 1) * HALF // LIST_ROWS]),
                y[r][h][:],
                wgo_t[:, cols],
                MULT,
            )

        Q = HALF // 2
        for i in range(3):
            for h in range(2):
                if i == 0 and h == 0:
                    gather(i, h, 0, P)
                    gather(i, h, P, HALF)
                else:
                    gather(i, h, 0, HALF)
                if i == 1:
                    interleave(nc.scalar.copy, 0, h, 0, HALF)
        gather(3, 0, 0, Q)
        interleave(nc.scalar.copy, 1, 0, 0, Q)
        gather(3, 0, Q + P, HALF)
        gather(3, 0, Q, Q + P)
        interleave(nc.scalar.copy, 1, 0, Q, Q + P)
        interleave(nc.vector.tensor_copy, 1, 0, Q + P, HALF)
        interleave_w(nc.vector.tensor_copy, 0)
        quantize(0, 0, Q)
        quantize_w(0)
        interleave_w(nc.scalar.copy, 1)
        quantize(0, Q, HALF)
        product(0, 0, 0, Q)
        product(0, 0, Q, HALF)
        gather(3, 1, 0, HALF)
        quantize_w(1)
        product(1, 0, 0, Q)
        product(1, 0, Q, HALF)
        interleave(nc.scalar.copy, 1, 1, 0, HALF)
        scatter(0, 0)
        quantize(1, 0, HALF)
        for r in range(2):
            product(r, 1, 0, HALF)
        scatter(1, 0)
        for r in range(2):
            scatter(r, 1)
            nc.sync.dma_start(out[r * P : (r + 1) * P, :], windows[r][:])
